import numpy as np
import ml_dtypes


def mxq(x, axis, fmt="e4m3"):
    dtype, down = {"e4m3": (ml_dtypes.float8_e4m3fn, 7), "e5m2": (ml_dtypes.float8_e5m2, 14)}[fmt]
    v = np.moveaxis(np.asarray(x, np.float32).astype(ml_dtypes.bfloat16).astype(np.float64), axis, -1)
    blocks = v.reshape(v.shape[:-1] + (-1, 32))
    amax = np.abs(blocks).max(-1, keepdims=True)
    byte = np.maximum(np.where(amax > 0, np.frexp(amax)[1] - 1 + 127, 0) - down, 1)
    scale = np.exp2(byte - 127.0)
    codes = (blocks / scale).astype(np.float32).astype(dtype).astype(np.float64)
    return np.moveaxis((codes * scale).reshape(v.shape), -1, axis)


WIDE = False


def mx_kscale(k):
    if not WIDE:
        return np.ones(k)
    levels = np.array([10, -10, 5, -5, 0])
    if k % 512:
        return np.exp2(np.random.permutation(np.resize(levels, k // 32))).repeat(32)
    a = np.empty((k // 512, 16))
    for p in range(k // 512):
        a[p, :8] = np.random.permutation(np.resize(levels, 8))
        for g in range(8):
            far = levels[np.abs(levels - a[p, g]) >= 10]
            a[p, g + 8] = far[np.random.randint(len(far))]
    return np.exp2(a.ravel()).repeat(32)


def f64(x):
    return np.asarray(x).astype(np.float64)


def striped(idx):
    return np.tile(idx.reshape(-1, 16).T, (8, 1)).astype(np.uint16)


def unstriped(offs):
    return offs[:16].T.reshape(-1).astype(np.int64)


def striped8(idx):
    return np.concatenate([x.reshape(-1, 16).T for x in idx]).astype(np.uint16)


def runs(offs, k):
    lists = np.stack([offs[16 * r : 16 * r + 16].T.reshape(-1) for r in range(8)]).astype(np.int64)
    return lists[np.arange(k) % 512 // 64]


def pack_weight(w):
    k, n = w.shape
    w = f64(np.asarray(w, np.float32).astype(ml_dtypes.bfloat16)).reshape(k // 32, 32, n)
    amax = np.abs(w).max(1)
    byte = np.clip(np.where(amax > 0, np.frexp(amax)[1] - 1 + 127 - 7, 1), 1, 254)
    scaled = (w * np.exp2(127.0 - byte)[:, None, :]).reshape(k, n).astype(np.float32)
    words = np.ascontiguousarray(scaled.reshape(k // 512, 128, 4, n).transpose(0, 1, 3, 2)).astype(ml_dtypes.float8_e4m3fn).view(np.uint8)
    return words, np.ascontiguousarray(byte.astype(np.uint8).reshape(k // 512, 16, n))


def unpack_weight(words, scales):
    g, p, n, _ = words.shape
    vals = np.ascontiguousarray(words).view(ml_dtypes.float8_e4m3fn).astype(np.float64) * np.repeat(np.exp2(scales.astype(np.float64) - 127.0), 8, axis=1)[..., None]
    return vals.transpose(0, 1, 3, 2).reshape(g * 512, n)


def sigmoid(v):
    return 1.0 / (1.0 + np.exp(-np.maximum(v, -700.0)))

def planes(y):
    n, m = y.shape
    v = y.astype(np.float32).astype(ml_dtypes.bfloat16).astype(np.float64).reshape(n // 32, 32, m)
    top = np.abs(v).max(1)
    byte = np.clip(np.where(top > 0, np.frexp(top)[1] - 1 + 127 - 7, 1), 1, 254)
    codes = (v * np.exp2(127.0 - byte)[:, None, :]).reshape(n, m).astype(np.float32).astype(ml_dtypes.float8_e4m3fn).view(np.uint8)
    words = codes.reshape(n // 512, 128, 4, m).transpose(0, 1, 3, 2)
    return np.ascontiguousarray(words), np.ascontiguousarray(byte.astype(np.uint8).reshape(n // 512, 16, m))


K, T, S, H, G = 512, 1024, 512, 512, 2048


def setup_inputs():
    n = np.random.standard_normal
    s = mx_kscale(K)[:, None]
    packed_xT = pack_weight(n((K, T)) * s)
    packed_w1 = pack_weight(n((K, H)) / np.sqrt(K) / s)
    packed_w2 = pack_weight(n((K, H)) / np.sqrt(K) / s)
    packed_dT = pack_weight(n((K, G)) / s)
    return {
        "x_words": packed_xT[0],
        "x_scales": packed_xT[1],
        "w1_words": packed_w1[0],
        "w1_scales": packed_w1[1],
        "w2_words": packed_w2[0],
        "w2_scales": packed_w2[1],
        "gs": (np.random.uniform(0.5, 1.5, (K, 1)) * s).astype(np.float32),
        "d_words": packed_dT[0],
        "d_scales": packed_dT[1],
        "offs": striped(np.random.permutation(T)[:S]),
        "two": striped(np.random.permutation(T)[:S]),
        "n1": striped8(np.stack([np.random.permutation(S) for _ in range(8)])),
        "n2": striped8(np.stack([np.random.permutation(S) for _ in range(8)])),
        "k1": striped8(np.random.randint(0, G, (8, H))),
        "n3": striped8(np.stack([np.random.permutation(S) for _ in range(8)])),
        "n4": striped8(np.stack([np.random.permutation(S) for _ in range(8)])),
    }


def reference(x_words, x_scales, w1_words, w1_scales, w2_words, w2_scales, gs, d_words, d_scales, offs, two, n1, n2, k1, n3, n4):
    d_k1 = unpack_weight(d_words, d_scales)[np.arange(K)[:, None], runs(k1, K)]
    xq = unpack_weight(x_words, x_scales)[:, unstriped(offs)]
    y = unpack_weight(w1_words, w1_scales).T @ xq
    x_two = unpack_weight(x_words, x_scales)[:, unstriped(two)]
    d = unpack_weight(w2_words, w2_scales).T @ x_two
    z = f64(gs) * (y * (sigmoid(d[np.arange(H)[:, None], runs(n2, H)])) - (0.5 * (y[np.arange(H)[:, None], runs(n1, H)])))
    h = 0.0625 * ((d_k1.T @ mxq(z, 0, "e4m3")))
    out_0 = 0.75 * ((h - (h[np.arange(H)[:, None], runs(n3, H)])) * (h - (h[np.arange(H)[:, None], runs(n4, H)])))
    return (out_0,) + planes(out_0)

@@ -1,0 +1,233 @@
+from contextlib import ExitStack
+
+import concourse.mybir as mybir
+
+K, T, S, H, G = 512, 1024, 512, 512, 2048
+FLOPS = 3 * 2 * 512 * 512 * 512
+
+F32 = mybir.dt.float32
+BF16 = mybir.dt.bfloat16
+U32 = mybir.dt.uint32
+I32 = mybir.dt.int32
+U16 = mybir.dt.uint16
+U8 = mybir.dt.uint8
+FP8X4 = mybir.dt.float8_e4m3fn_x4
+ALU = mybir.AluOpType
+ACT = mybir.ActivationFunctionType
+
+P = 128
+PACK = 4
+Z_CHUNKS = ((0, 256), (256, 512))
+OUT_CHUNKS = ((0, 256), (256, 512))
+
+
+def deal(nc, dst, src):
+    nc.vector.tensor_copy(
+        out=dst.rearrange("p (t m) -> p m t", t=PACK),
+        in_=src.rearrange("p (m t) -> p m t", t=PACK),
+    )
+
+
+def words_view(words):
+    return words[0].rearrange("p n r -> p (n r)").bitcast(I32)
+
+
+def entries(offsets, lo, hi):
+    return offsets[:, lo // 16 : hi // 16]
+
+
+def tile_picked_twqgatebquad_none_po_kernel(
+    tc, x_words, x_scales, w1_words, w1_scales, w2_words, w2_scales, gs, d_words, d_scales,
+    offs, two, n1, n2, k1, n3, n4, out_0, out_1, out_2,
+):
+    nc = tc.nc
+    with ExitStack() as ctx:
+        lists = ctx.enter_context(tc.tile_pool(name="lists", bufs=1))
+        keep = ctx.enter_context(tc.tile_pool(name="keep", bufs=1))
+        psum = ctx.enter_context(tc.psum_pool(name="psum", bufs=1))
+
+        def sb(name, shape, dtype):
+            return keep.tile(shape, dtype, name=name, align_bytes=64)
+
+        def load_list(name, src):
+            tile = lists.tile([P, S // 16], U16, name=name)
+            nc.sync.dma_start(tile[:], src)
+            return tile
+
+        def load_scale_rows(queue, tile, first, scales):
+            for q in range(4):
+                queue.dma_start(
+                    out=tile[32 * q + first : 32 * q + first + 4, :].bitcast(I32),
+                    in_=scales[0, 4 * q : 4 * q + 4, :].bitcast(I32),
+                )
+
+        x_w = sb("x_w", [P, T], U32)
+        x_s = sb("x_s", [P, T], U8)
+        w_s = sb("w_s", [P, H], U8)
+        d_s = sb("d_s", [P, G], U8)
+        c_s = sb("c_s", [P, H], U8)
+        nc.gpsimd.memset(x_s[:].bitcast(I32), 0)
+        nc.gpsimd.memset(w_s[:].bitcast(I32), 0)
+        nc.gpsimd.memset(d_s[:].bitcast(I32), 0)
+        nc.gpsimd.memset(c_s[:].bitcast(I32), 0)
+
+        two_l = load_list("two_l", two)
+        load_scale_rows(nc.sync, x_s, 0, x_scales)
+        nc.sync.dma_start(out=x_w[:].bitcast(I32), in_=words_view(x_words))
+        w2_w = sb("w2_w", [P, H], U32)
+        nc.sync.dma_start(out=w2_w[:].bitcast(I32), in_=words_view(w2_words))
+        load_scale_rows(nc.scalar, w_s, 0, w2_scales)
+        load_scale_rows(nc.scalar, w_s, 4, w1_scales)
+        offs_l = load_list("offs_l", offs)
+        w1_w = sb("w1_w", [P, H], U32)
+        nc.sync.dma_start(out=w1_w[:].bitcast(I32), in_=words_view(w1_words))
+        n2_l = load_list("n2_l", n2)
+        gs_t = sb("gs_t", [P, PACK], F32)
+        nc.sync.dma_start(out=gs_t[:], in_=gs.rearrange("(p t) o -> p (t o)", t=PACK))
+        d_w = sb("d_w", [P, G], U32)
+        nc.sync.dma_start(out=d_w[:].bitcast(I32), in_=words_view(d_words))
+        k1_l = load_list("k1_l", k1)
+        d_rows = d_scales[0].rearrange("(r e) c -> e r c", e=2)
+        for e in range(2):
+            nc.sync.dma_start(out=d_s[e:P:16, :].bitcast(I32), in_=d_rows[e].bitcast(I32))
+        n1_l = load_list("n1_l", n1)
+        n3_l = load_list("n3_l", n3)
+        n4_l = load_list("n4_l", n4)
+
+        def pick(name, window, offsets, dtype):
+            tile = sb(name, [P, S], dtype)
+            nc.vector.tensor_copy(out=tile[:], in_=window[:].indirect(offsets[:]))
+            return tile
+
+        def product(banks, lhs_w, lhs_s, rhs_w, rhs_s, lo, hi, t):
+            cols = slice(P * t, P * (t + 1))
+            nc.tensor.matmul_mx(
+                out=banks[t][:, lo:hi],
+                lhsT=lhs_w[:, cols].bitcast(FP8X4),
+                lhsT_scale=lhs_s[:, cols],
+                rhs=rhs_w.bitcast(FP8X4),
+                rhs_scale=rhs_s,
+                start=True,
+                stop=True,
+            )
+
+        banks_a = [psum.tile([P, S], F32, name="bank_a%d" % t) for t in range(PACK)]
+        banks_b = [psum.tile([P, S], F32, name="bank_b%d" % t) for t in range(PACK)]
+
+        x2_s = pick("x2_s", x_s, two_l, U8)
+        x2_w = pick("x2_w", x_w, two_l, U32)
+        w2_d = sb("w2_d", [P, H], U32)
+        deal(nc, w2_d[:], w2_w[:])
+        ws_d = sb("ws_d", [P, H], U8)
+        deal(nc, ws_d[:], w_s[:])
+        d_win = []
+        for t in range(PACK):
+            product(banks_a, w2_d, ws_d, x2_w[:], x2_s[:], 0, S, t)
+            win = sb("d_win%d" % t, [P, S], F32)
+            nc.scalar.activation(out=win[:], in_=banks_a[t][:], func=ACT.Copy)
+            d_win.append(win)
+
+        gates = [sb("gate%d" % c, [P, PACK, hi - lo], F32) for c, (lo, hi) in enumerate(Z_CHUNKS)]
+
+        def gather_gates(c):
+            lo, hi = Z_CHUNKS[c]
+            for t in range(PACK):
+                nc.scalar.activation(
+                    out=gates[c][:, t, :], in_=d_win[t][:].indirect(entries(n2_l, lo, hi)), func=ACT.Sigmoid
+                )
+
+        gather_gates(0)
+        half_gs = sb("half_gs", [P, PACK], F32)
+        nc.gpsimd.tensor_scalar(out=half_gs[:], in0=gs_t[:], scalar1=-0.5, scalar2=0.0, op0=ALU.mult, op1=ALU.add)
+
+        x1_w = pick("x1_w", x_w, offs_l, U32)
+        x1_s = pick("x1_s", x_s, offs_l, U8)
+        w1_d = sb("w1_d", [P, H], U32)
+        deal(nc, w1_d[:], w1_w[:])
+        y_win = []
+        for t in range(PACK):
+            product(banks_b, w1_d, ws_d[4:P, :], x1_w[:], x1_s[:], 0, S, t)
+            win = sb("y_win%d" % t, [P, S], F32)
+            nc.scalar.activation(out=win[:], in_=banks_b[t][:], func=ACT.Copy, scale=half_gs[:, t : t + 1])
+            y_win.append(win)
+
+        c_wg = pick("c_wg", d_w, k1_l, U32)
+        c_sg = pick("c_sg", d_s, k1_l, U8)
+        c_w = sb("c_w", [P, H], U32)
+        deal(nc, c_w[:], c_wg[:])
+        c_sd = sb("c_sd", [P, H], U8)
+        deal(nc, c_sd[:], c_sg[:])
+        for r in range(4):
+            src = 16 * (r // 2) + r % 2
+            nc.sync.dma_start(out=c_s[r:P:32, :].bitcast(I32), in_=c_sd[src:P:32, :].bitcast(I32))
+
+        h_win = [sb("h_win%d" % t, [P, S], F32) for t in range(PACK)]
+        h_own = [sb("h_own%d" % t, [P, S], F32) for t in range(PACK)]
+        for c, (lo, hi) in enumerate(Z_CHUNKS):
+            width = hi - lo
+            if c > 0:
+                gather_gates(c)
+            gated = sb("gated%d" % c, [P, PACK, width], F32)
+            z_f = sb("z_f%d" % c, [P, PACK, width], F32)
+            for t in range(PACK):
+                nc.vector.scalar_tensor_tensor(
+                    out=gated[:, t, :], in0=banks_b[t][:, lo:hi], scalar=gs_t[:, t : t + 1], in1=gates[c][:, t, :],
+                    op0=ALU.mult, op1=ALU.mult,
+                )
+            for t in range(PACK):
+                nc.vector.tensor_tensor(
+                    out=z_f[:, t, :], in0=y_win[t][:].indirect(entries(n1_l, lo, hi)), in1=gated[:, t, :], op=ALU.add
+                )
+            z_bf = sb("z_bf%d" % c, [P, width * PACK], BF16)
+            z_dst = z_bf[:].rearrange("p (c i t) -> p c t i", i=4, t=PACK)
+            z_src = z_f[:].rearrange("p t (c i) -> p c t i", i=4)
+            if c + 1 < len(Z_CHUNKS):
+                nc.scalar.copy(out=z_dst, in_=z_src)
+            else:
+                nc.vector.tensor_copy(out=z_dst, in_=z_src)
+            z_w = sb("z_w%d" % c, [P, width], U32)
+            z_s = sb("z_s%d" % c, [P, width], U8)
+            nc.vector.quantize_mx(out=z_w[:].bitcast(FP8X4), scales=z_s[:], in_=z_bf[:])
+            for t in range(PACK):
+                product(banks_a, c_w, c_s, z_w[:], z_s[:], lo, hi, t)
+                nc.scalar.activation(out=h_win[t][:, lo:hi], in_=banks_a[t][:, lo:hi], func=ACT.Copy, scale=0.0625)
+            for t in range(PACK):
+                nc.scalar.activation(out=h_own[t][:, lo:hi], in_=banks_a[t][:, lo:hi], func=ACT.Copy, scale=0.0625)
+
+        out_rows = out_0.rearrange("(p t) j -> p t j", t=PACK)
+        out_words = words_view(out_1)
+        o_s = sb("o_s", [P, S], U8)
+        for c, (lo, hi) in enumerate(OUT_CHUNKS):
+            width = hi - lo
+            first = sb("first%d" % c, [P, PACK, width], F32)
+            second = sb("second%d" % c, [P, PACK, width], F32)
+            for t in range(PACK):
+                nc.vector.tensor_tensor(
+                    out=first[:, t, :], in0=h_win[t][:].indirect(entries(n3_l, lo, hi)),
+                    in1=h_own[t][:, lo:hi], op=ALU.subtract,
+                )
+                nc.vector.tensor_tensor(
+                    out=second[:, t, :], in0=h_win[t][:].indirect(entries(n4_l, lo, hi)),
+                    in1=h_own[t][:, lo:hi], op=ALU.subtract,
+                )
+            o_f = sb("o_f%d" % c, [P, PACK, width], F32)
+            nc.vector.scalar_tensor_tensor(
+                out=o_f[:].rearrange("p t j -> p (t j)"), in0=first[:].rearrange("p t j -> p (t j)"), scalar=0.75,
+                in1=second[:].rearrange("p t j -> p (t j)"), op0=ALU.mult, op1=ALU.mult,
+            )
+            nc.sync.dma_start(out=out_rows[:, :, lo:hi], in_=o_f[:])
+            o_bf = sb("o_bf%d" % c, [P, width * PACK], BF16)
+            o_dst = o_bf[:].rearrange("p (c i t) -> p c t i", i=4, t=PACK)
+            o_src = o_f[:].rearrange("p t (c i) -> p c t i", i=4)
+            if c + 1 < len(OUT_CHUNKS):
+                nc.scalar.copy(out=o_dst, in_=o_src)
+            else:
+                nc.vector.tensor_copy(out=o_dst, in_=o_src)
+            o_w = sb("o_w%d" % c, [P, width], U32)
+            nc.vector.quantize_mx(out=o_w[:].bitcast(FP8X4), scales=o_s[:, lo:hi], in_=o_bf[:])
+            nc.sync.dma_start(out=out_words[:, lo:hi], in_=o_w[:].bitcast(I32))
+        for q in range(4):
+            queue = nc.scalar if q % 2 else nc.sync
+            queue.dma_start(
+                out=out_2[0, 4 * q : 4 * q + 4, :].bitcast(I32), in_=o_s[32 * q : 32 * q + 4, :].bitcast(I32)
+            )

@@ -17,8 +17,6 @@ ACT = mybir.ActivationFunctionType
 
 P = 128
 PACK = 4
-Z_CHUNKS = ((0, 256), (256, 512))
-OUT_CHUNKS = ((0, 256), (256, 512))
 
 
 def deal(nc, dst, src):
@@ -46,19 +44,21 @@ def tile_picked_twqgatebquad_none_po_kernel(
         keep = ctx.enter_context(tc.tile_pool(name="keep", bufs=1))
         psum = ctx.enter_context(tc.psum_pool(name="psum", bufs=1))
 
-        def sb(name, shape, dtype):
-            return keep.tile(shape, dtype, name=name, align_bytes=64)
+        def sb(name, shape, dtype, tag=None):
+            return keep.tile(shape, dtype, name=name, tag=tag or name, align_bytes=64)
 
         def load_list(name, src):
             tile = lists.tile([P, S // 16], U16, name=name)
             nc.sync.dma_start(tile[:], src)
             return tile
 
-        def load_scale_rows(queue, tile, first, scales):
-            for q in range(4):
-                queue.dma_start(
-                    out=tile[32 * q + first : 32 * q + first + 4, :].bitcast(I32),
-                    in_=scales[0, 4 * q : 4 * q + 4, :].bitcast(I32),
+        def load_scale_rows(tile, first, planes, scales, which):
+            rows = scales[0].bitcast(I32).rearrange("(q r) c -> r q c", r=4)
+            step = 4 * planes
+            for r in which:
+                nc.sync.dma_start(
+                    out=tile[first + r : P : step, :].bitcast(I32),
+                    in_=rows[r].unsqueeze(1).to_broadcast([4, 32 // step, rows.shape[2]]),
                 )
 
         x_w = sb("x_w", [P, T], U32)
@@ -66,30 +66,33 @@ def tile_picked_twqgatebquad_none_po_kernel(
         w_s = sb("w_s", [P, H], U8)
         d_s = sb("d_s", [P, G], U8)
         c_s = sb("c_s", [P, H], U8)
-        nc.gpsimd.memset(x_s[:].bitcast(I32), 0)
-        nc.gpsimd.memset(w_s[:].bitcast(I32), 0)
         nc.gpsimd.memset(d_s[:].bitcast(I32), 0)
+        d_win = [sb("d_win%d" % t, [P, 2 * S], F32) for t in range(PACK)]
+        for t in range(PACK):
+            nc.gpsimd.memset(d_win[t][:, S:], 0.0)
+
         nc.gpsimd.memset(c_s[:].bitcast(I32), 0)
 
         two_l = load_list("two_l", two)
-        load_scale_rows(nc.sync, x_s, 0, x_scales)
+        load_scale_rows(x_s, 0, 1, x_scales, range(4))
+        load_scale_rows(w_s, 0, 2, w2_scales, (0, 1))
         nc.sync.dma_start(out=x_w[:].bitcast(I32), in_=words_view(x_words))
         w2_w = sb("w2_w", [P, H], U32)
         nc.sync.dma_start(out=w2_w[:].bitcast(I32), in_=words_view(w2_words))
-        load_scale_rows(nc.scalar, w_s, 0, w2_scales)
-        load_scale_rows(nc.scalar, w_s, 4, w1_scales)
+        load_scale_rows(w_s, 0, 2, w2_scales, (2, 3))
+        load_scale_rows(w_s, 4, 2, w1_scales, range(4))
         offs_l = load_list("offs_l", offs)
         w1_w = sb("w1_w", [P, H], U32)
         nc.sync.dma_start(out=w1_w[:].bitcast(I32), in_=words_view(w1_words))
         n2_l = load_list("n2_l", n2)
         gs_t = sb("gs_t", [P, PACK], F32)
         nc.sync.dma_start(out=gs_t[:], in_=gs.rearrange("(p t) o -> p (t o)", t=PACK))
-        d_w = sb("d_w", [P, G], U32)
-        nc.sync.dma_start(out=d_w[:].bitcast(I32), in_=words_view(d_words))
         k1_l = load_list("k1_l", k1)
         d_rows = d_scales[0].rearrange("(r e) c -> e r c", e=2)
         for e in range(2):
             nc.sync.dma_start(out=d_s[e:P:16, :].bitcast(I32), in_=d_rows[e].bitcast(I32))
+        d_w = sb("d_w", [P, G], U32)
+        nc.sync.dma_start(out=d_w[:].bitcast(I32), in_=words_view(d_words))
         n1_l = load_list("n1_l", n1)
         n3_l = load_list("n3_l", n3)
         n4_l = load_list("n4_l", n4)
@@ -120,112 +123,135 @@ def tile_picked_twqgatebquad_none_po_kernel(
         deal(nc, w2_d[:], w2_w[:])
         ws_d = sb("ws_d", [P, H], U8)
         deal(nc, ws_d[:], w_s[:])
-        d_win = []
         for t in range(PACK):
             product(banks_a, w2_d, ws_d, x2_w[:], x2_s[:], 0, S, t)
-            win = sb("d_win%d" % t, [P, S], F32)
-            nc.scalar.activation(out=win[:], in_=banks_a[t][:], func=ACT.Copy)
-            d_win.append(win)
 
-        gates = [sb("gate%d" % c, [P, PACK, hi - lo], F32) for c, (lo, hi) in enumerate(Z_CHUNKS)]
-
-        def gather_gates(c):
-            lo, hi = Z_CHUNKS[c]
-            for t in range(PACK):
-                nc.scalar.activation(
-                    out=gates[c][:, t, :], in_=d_win[t][:].indirect(entries(n2_l, lo, hi)), func=ACT.Sigmoid
-                )
-
-        gather_gates(0)
-        half_gs = sb("half_gs", [P, PACK], F32)
-        nc.gpsimd.tensor_scalar(out=half_gs[:], in0=gs_t[:], scalar1=-0.5, scalar2=0.0, op0=ALU.mult, op1=ALU.add)
-
-        x1_w = pick("x1_w", x_w, offs_l, U32)
         x1_s = pick("x1_s", x_s, offs_l, U8)
+        x1_w = pick("x1_w", x_w, offs_l, U32)
         w1_d = sb("w1_d", [P, H], U32)
         deal(nc, w1_d[:], w1_w[:])
-        y_win = []
+        half_gs = sb("half_gs", [P, PACK], F32)
+        nc.vector.tensor_scalar(out=half_gs[:], in0=gs_t[:], scalar1=-0.5, scalar2=0.0, op0=ALU.mult, op1=ALU.add)
         for t in range(PACK):
             product(banks_b, w1_d, ws_d[4:P, :], x1_w[:], x1_s[:], 0, S, t)
-            win = sb("y_win%d" % t, [P, S], F32)
-            nc.scalar.activation(out=win[:], in_=banks_b[t][:], func=ACT.Copy, scale=half_gs[:, t : t + 1])
-            y_win.append(win)
+        win = [sb("win%d" % t, [P, 2 * S], F32) for t in range(PACK)]
 
-        c_wg = pick("c_wg", d_w, k1_l, U32)
+        def gate(t):
+            nc.scalar.activation(out=d_win[t][:, :S], in_=banks_a[t][:], func=ACT.Copy)
+            nc.scalar.activation(out=win[t][:, S:], in_=d_win[t][:].indirect(n2_l[:]), func=ACT.Sigmoid)
+
+        def fetch_y(t):
+            nc.scalar.activation(out=win[t][:, :S], in_=banks_b[t][:], func=ACT.Copy, scale=half_gs[:, t : t + 1])
+
+        gate(0)
+        gate(1)
+        fetch_y(0)
+        fetch_y(1)
+        for t in (2, 3):
+            gate(t)
+            fetch_y(t)
+
         c_sg = pick("c_sg", d_s, k1_l, U8)
-        c_w = sb("c_w", [P, H], U32)
-        deal(nc, c_w[:], c_wg[:])
         c_sd = sb("c_sd", [P, H], U8)
         deal(nc, c_sd[:], c_sg[:])
         for r in range(4):
             src = 16 * (r // 2) + r % 2
             nc.sync.dma_start(out=c_s[r:P:32, :].bitcast(I32), in_=c_sd[src:P:32, :].bitcast(I32))
+        c_wg = pick("c_wg", d_w, k1_l, U32)
+        c_w = sb("c_w", [P, H], U32)
+        deal(nc, c_w[:], c_wg[:])
 
-        h_win = [sb("h_win%d" % t, [P, S], F32) for t in range(PACK)]
+        mid = S // 2
+        halves = ((0, mid), (mid, S))
+        copies = (nc.scalar.copy, nc.vector.tensor_copy)
+
+        def quantise_half(name, src, h, words, scales, tag=None):
+            lo, hi = halves[h]
+            grouped = sb("%s_bf%d" % (name, h), [P, mid * PACK], BF16, tag=tag)
+            copies[h](
+                out=grouped[:].rearrange("p (c i t) -> p c t i", i=4, t=PACK),
+                in_=src[:, :, lo:hi].rearrange("p t (c i) -> p c t i", i=4),
+            )
+            nc.vector.quantize_mx(out=words.bitcast(FP8X4), scales=scales, in_=grouped[:])
+
+        z_f = sb("z_f", [P, PACK, S], F32)
+        gated = sb("gated", [P, PACK, S], F32, tag="c_wg")
+
+        def gate_y(t):
+            nc.vector.scalar_tensor_tensor(
+                out=gated[:, t, :], in0=banks_b[t][:], scalar=gs_t[:, t : t + 1], in1=win[t][:, S:],
+                op0=ALU.mult, op1=ALU.mult,
+            )
+
+        def mix(t, lo, hi):
+            nc.vector.tensor_tensor(
+                out=z_f[:, t, lo:hi], in0=win[t][:].indirect(entries(n1_l, lo, hi)), in1=gated[:, t, lo:hi], op=ALU.add
+            )
+
+        h_win = d_win
         h_own = [sb("h_own%d" % t, [P, S], F32) for t in range(PACK)]
-        for c, (lo, hi) in enumerate(Z_CHUNKS):
-            width = hi - lo
-            if c > 0:
-                gather_gates(c)
-            gated = sb("gated%d" % c, [P, PACK, width], F32)
-            z_f = sb("z_f%d" % c, [P, PACK, width], F32)
-            for t in range(PACK):
-                nc.vector.scalar_tensor_tensor(
-                    out=gated[:, t, :], in0=banks_b[t][:, lo:hi], scalar=gs_t[:, t : t + 1], in1=gates[c][:, t, :],
-                    op0=ALU.mult, op1=ALU.mult,
-                )
-            for t in range(PACK):
-                nc.vector.tensor_tensor(
-                    out=z_f[:, t, :], in0=y_win[t][:].indirect(entries(n1_l, lo, hi)), in1=gated[:, t, :], op=ALU.add
-                )
-            z_bf = sb("z_bf%d" % c, [P, width * PACK], BF16)
-            z_dst = z_bf[:].rearrange("p (c i t) -> p c t i", i=4, t=PACK)
-            z_src = z_f[:].rearrange("p t (c i) -> p c t i", i=4)
-            if c + 1 < len(Z_CHUNKS):
-                nc.scalar.copy(out=z_dst, in_=z_src)
-            else:
-                nc.vector.tensor_copy(out=z_dst, in_=z_src)
-            z_w = sb("z_w%d" % c, [P, width], U32)
-            z_s = sb("z_s%d" % c, [P, width], U8)
-            nc.vector.quantize_mx(out=z_w[:].bitcast(FP8X4), scales=z_s[:], in_=z_bf[:])
-            for t in range(PACK):
-                product(banks_a, c_w, c_s, z_w[:], z_s[:], lo, hi, t)
-                nc.scalar.activation(out=h_win[t][:, lo:hi], in_=banks_a[t][:, lo:hi], func=ACT.Copy, scale=0.0625)
-            for t in range(PACK):
-                nc.scalar.activation(out=h_own[t][:, lo:hi], in_=banks_a[t][:, lo:hi], func=ACT.Copy, scale=0.0625)
+
+        last = PACK - 1
+        for t in range(last):
+            gate_y(t)
+            mix(t, 0, S)
+        gate_y(last)
+        z_w = sb("z_w", [P, S], U32)
+        z_s = sb("z_s", [P, S], U8)
+        for h, (lo, hi) in enumerate(halves):
+            mix(last, lo, hi)
+            quantise_half("z", z_f, h, z_w[:, lo:hi], z_s[:, lo:hi])
+        product(banks_a, c_w, c_s, z_w[:, :mid], z_s[:, :mid], 0, mid, 0)
+        product(banks_b, c_w, c_s, z_w[:, mid:], z_s[:, mid:], mid, S, 0)
+        for dst in (h_win[0], h_own[0]):
+            nc.scalar.activation(out=dst[:, :mid], in_=banks_a[0][:, :mid], func=ACT.Copy, scale=0.0625)
+            nc.vector.tensor_scalar(
+                out=dst[:, mid:S], in0=banks_b[0][:, mid:], scalar1=0.0625, scalar2=None, op0=ALU.mult
+            )
+        for t in range(1, PACK):
+            product(banks_a, c_w, c_s, z_w[:], z_s[:], 0, S, t)
+            for dst in (h_win[t], h_own[t]):
+                nc.scalar.activation(out=dst[:, :S], in_=banks_a[t][:], func=ACT.Copy, scale=0.0625)
 
         out_rows = out_0.rearrange("(p t) j -> p t j", t=PACK)
         out_words = words_view(out_1)
+        first = sb("first", [P, PACK, S], F32)
+        second = sb("second", [P, PACK, S], F32)
+        o_f = sb("o_f", [P, PACK, S], F32)
         o_s = sb("o_s", [P, S], U8)
-        for c, (lo, hi) in enumerate(OUT_CHUNKS):
-            width = hi - lo
-            first = sb("first%d" % c, [P, PACK, width], F32)
-            second = sb("second%d" % c, [P, PACK, width], F32)
-            for t in range(PACK):
+
+        def differences(t, lo, hi):
+            for dst, offsets in ((first, n3_l), (second, n4_l)):
                 nc.vector.tensor_tensor(
-                    out=first[:, t, :], in0=h_win[t][:].indirect(entries(n3_l, lo, hi)),
+                    out=dst[:, t, lo:hi], in0=h_win[t][:].indirect(entries(offsets, lo, hi)),
                     in1=h_own[t][:, lo:hi], op=ALU.subtract,
                 )
-                nc.vector.tensor_tensor(
-                    out=second[:, t, :], in0=h_win[t][:].indirect(entries(n4_l, lo, hi)),
-                    in1=h_own[t][:, lo:hi], op=ALU.subtract,
-                )
-            o_f = sb("o_f%d" % c, [P, PACK, width], F32)
+
+        def result(t, lo, hi):
             nc.vector.scalar_tensor_tensor(
-                out=o_f[:].rearrange("p t j -> p (t j)"), in0=first[:].rearrange("p t j -> p (t j)"), scalar=0.75,
-                in1=second[:].rearrange("p t j -> p (t j)"), op0=ALU.mult, op1=ALU.mult,
+                out=o_f[:, t, lo:hi], in0=first[:, t, lo:hi], scalar=0.75, in1=second[:, t, lo:hi],
+                op0=ALU.mult, op1=ALU.mult,
             )
-            nc.sync.dma_start(out=out_rows[:, :, lo:hi], in_=o_f[:])
-            o_bf = sb("o_bf%d" % c, [P, width * PACK], BF16)
-            o_dst = o_bf[:].rearrange("p (c i t) -> p c t i", i=4, t=PACK)
-            o_src = o_f[:].rearrange("p t (c i) -> p c t i", i=4)
-            if c + 1 < len(OUT_CHUNKS):
-                nc.scalar.copy(out=o_dst, in_=o_src)
-            else:
-                nc.vector.tensor_copy(out=o_dst, in_=o_src)
-            o_w = sb("o_w%d" % c, [P, width], U32)
-            nc.vector.quantize_mx(out=o_w[:].bitcast(FP8X4), scales=o_s[:, lo:hi], in_=o_bf[:])
+            nc.sync.dma_start(out=out_rows[:, t, lo:hi], in_=o_f[:, t, lo:hi])
+
+        def planes(h):
+            lo, hi = halves[h]
+            o_w = sb("o_w%d" % h, [P, mid], U32)
+            quantise_half("o", o_f, h, o_w[:], o_s[:, lo:hi], tag="o_bf")
             nc.sync.dma_start(out=out_words[:, lo:hi], in_=o_w[:].bitcast(I32))
+
+        differences(0, mid, S)
+        differences(0, 0, mid)
+        for t in range(1, last):
+            differences(t, 0, S)
+            result(t - 1, 0, S)
+        differences(last, 0, mid)
+        result(last - 1, 0, S)
+        result(last, 0, mid)
+        planes(0)
+        differences(last, mid, S)
+        result(last, mid, S)
+        planes(1)
         for q in range(4):
             queue = nc.scalar if q % 2 else nc.sync
             queue.dma_start(

@@ -52,13 +52,11 @@ def tile_picked_twqgatebquad_none_po_kernel(
             nc.sync.dma_start(tile[:], src)
             return tile
 
-        def load_scale_rows(tile, first, planes, scales, which):
-            rows = scales[0].bitcast(I32).rearrange("(q r) c -> r q c", r=4)
-            step = 4 * planes
-            for r in which:
+        def load_scale_rows(tile, first, scales, which):
+            for q in which:
                 nc.sync.dma_start(
-                    out=tile[first + r : P : step, :].bitcast(I32),
-                    in_=rows[r].unsqueeze(1).to_broadcast([4, 32 // step, rows.shape[2]]),
+                    out=tile[32 * q + first : 32 * q + first + 4, :].bitcast(I32),
+                    in_=scales[0, 4 * q : 4 * q + 4, :].bitcast(I32),
                 )
 
         x_w = sb("x_w", [P, T], U32)
@@ -66,21 +64,26 @@ def tile_picked_twqgatebquad_none_po_kernel(
         w_s = sb("w_s", [P, H], U8)
         d_s = sb("d_s", [P, G], U8)
         c_s = sb("c_s", [P, H], U8)
-        nc.gpsimd.memset(d_s[:].bitcast(I32), 0)
+        nc.gpsimd.memset(w_s[:].bitcast(I32), 0)
+        nc.vector.memset(d_s[:].bitcast(I32), 0)
         d_win = [sb("d_win%d" % t, [P, 2 * S], F32) for t in range(PACK)]
         for t in range(PACK):
-            nc.gpsimd.memset(d_win[t][:, S:], 0.0)
+            nc.vector.memset(d_win[t][:, S:], 0.0)
 
         nc.gpsimd.memset(c_s[:].bitcast(I32), 0)
 
         two_l = load_list("two_l", two)
-        load_scale_rows(x_s, 0, 1, x_scales, range(4))
-        load_scale_rows(w_s, 0, 2, w2_scales, (0, 1))
+        for q in range(4):
+            rows = x_scales[0, 4 * q : 4 * q + 4, :].bitcast(I32)
+            nc.sync.dma_start(
+                out=x_s[32 * q : 32 * (q + 1), :].bitcast(I32), in_=rows.unsqueeze(0).to_broadcast([8, 4, T // 4])
+            )
+        load_scale_rows(w_s, 0, w2_scales, (0, 1))
         nc.sync.dma_start(out=x_w[:].bitcast(I32), in_=words_view(x_words))
         w2_w = sb("w2_w", [P, H], U32)
         nc.sync.dma_start(out=w2_w[:].bitcast(I32), in_=words_view(w2_words))
-        load_scale_rows(w_s, 0, 2, w2_scales, (2, 3))
-        load_scale_rows(w_s, 4, 2, w1_scales, range(4))
+        load_scale_rows(w_s, 0, w2_scales, (2, 3))
+        load_scale_rows(w_s, 4, w1_scales, range(4))
         offs_l = load_list("offs_l", offs)
         w1_w = sb("w1_w", [P, H], U32)
         nc.sync.dma_start(out=w1_w[:].bitcast(I32), in_=words_view(w1_words))

from contextlib import ExitStack

import concourse.mybir as mybir

K, T, S, H, G = 512, 1024, 512, 512, 2048
FLOPS = 3 * 2 * 512 * 512 * 512

F32 = mybir.dt.float32
BF16 = mybir.dt.bfloat16
U32 = mybir.dt.uint32
I32 = mybir.dt.int32
U16 = mybir.dt.uint16
U8 = mybir.dt.uint8
FP8X4 = mybir.dt.float8_e4m3fn_x4
ALU = mybir.AluOpType
ACT = mybir.ActivationFunctionType

P = 128
PACK = 4


def deal(nc, dst, src):
    nc.vector.tensor_copy(
        out=dst.rearrange("p (t m) -> p m t", t=PACK),
        in_=src.rearrange("p (m t) -> p m t", t=PACK),
    )


def words_view(words):
    return words[0].rearrange("p n r -> p (n r)").bitcast(I32)


def entries(offsets, lo, hi):
    return offsets[:, lo // 16 : hi // 16]


def tile_picked_twqgatebquad_none_po_kernel(
    tc, x_words, x_scales, w1_words, w1_scales, w2_words, w2_scales, gs, d_words, d_scales,
    offs, two, n1, n2, k1, n3, n4, out_0, out_1, out_2,
):
    nc = tc.nc
    with ExitStack() as ctx:
        lists = ctx.enter_context(tc.tile_pool(name="lists", bufs=1))
        keep = ctx.enter_context(tc.tile_pool(name="keep", bufs=1))
        psum = ctx.enter_context(tc.psum_pool(name="psum", bufs=1))

        def sb(name, shape, dtype, tag=None):
            return keep.tile(shape, dtype, name=name, tag=tag or name, align_bytes=64)

        def load_list(name, src):
            tile = lists.tile([P, S // 16], U16, name=name)
            nc.sync.dma_start(tile[:], src)
            return tile

        def load_scale_rows(tile, first, scales, which):
            for q in which:
                nc.sync.dma_start(
                    out=tile[32 * q + first : 32 * q + first + 4, :].bitcast(I32),
                    in_=scales[0, 4 * q : 4 * q + 4, :].bitcast(I32),
                )

        x_w = sb("x_w", [P, T], U32)
        x_s = sb("x_s", [P, T], U8)
        w_s = sb("w_s", [P, H], U8)
        d_s = sb("d_s", [P, G], U8)
        c_s = sb("c_s", [P, H], U8)
        nc.gpsimd.memset(w_s[:].bitcast(I32), 0)
        nc.vector.memset(d_s[:].bitcast(I32), 0)
        d_win = [sb("d_win%d" % t, [P, 2 * S], F32) for t in range(PACK)]
        for t in range(PACK):
            nc.vector.memset(d_win[t][:, S:], 0.0)

        nc.gpsimd.memset(c_s[:].bitcast(I32), 0)

        two_l = load_list("two_l", two)
        for q in range(4):
            rows = x_scales[0, 4 * q : 4 * q + 4, :].bitcast(I32)
            nc.sync.dma_start(
                out=x_s[32 * q : 32 * (q + 1), :].bitcast(I32), in_=rows.unsqueeze(0).to_broadcast([8, 4, T // 4])
            )
        load_scale_rows(w_s, 0, w2_scales, (0, 1))
        nc.sync.dma_start(out=x_w[:].bitcast(I32), in_=words_view(x_words))
        w2_w = sb("w2_w", [P, H], U32)
        nc.sync.dma_start(out=w2_w[:].bitcast(I32), in_=words_view(w2_words))
        load_scale_rows(w_s, 0, w2_scales, (2, 3))
        load_scale_rows(w_s, 4, w1_scales, range(4))
        offs_l = load_list("offs_l", offs)
        w1_w = sb("w1_w", [P, H], U32)
        nc.sync.dma_start(out=w1_w[:].bitcast(I32), in_=words_view(w1_words))
        n2_l = load_list("n2_l", n2)
        gs_t = sb("gs_t", [P, PACK], F32)
        nc.sync.dma_start(out=gs_t[:], in_=gs.rearrange("(p t) o -> p (t o)", t=PACK))
        k1_l = load_list("k1_l", k1)
        d_rows = d_scales[0].rearrange("(r e) c -> e r c", e=2)
        for e in range(2):
            nc.sync.dma_start(out=d_s[e:P:16, :].bitcast(I32), in_=d_rows[e].bitcast(I32))
        d_w = sb("d_w", [P, G], U32)
        nc.sync.dma_start(out=d_w[:].bitcast(I32), in_=words_view(d_words))
        n1_l = load_list("n1_l", n1)
        n3_l = load_list("n3_l", n3)
        n4_l = load_list("n4_l", n4)

        def pick(name, window, offsets, dtype):
            tile = sb(name, [P, S], dtype)
            nc.vector.tensor_copy(out=tile[:], in_=window[:].indirect(offsets[:]))
            return tile

        def product(banks, lhs_w, lhs_s, rhs_w, rhs_s, lo, hi, t):
            cols = slice(P * t, P * (t + 1))
            nc.tensor.matmul_mx(
                out=banks[t][:, lo:hi],
                lhsT=lhs_w[:, cols].bitcast(FP8X4),
                lhsT_scale=lhs_s[:, cols],
                rhs=rhs_w.bitcast(FP8X4),
                rhs_scale=rhs_s,
                start=True,
                stop=True,
            )

        banks_a = [psum.tile([P, S], F32, name="bank_a%d" % t) for t in range(PACK)]
        banks_b = [psum.tile([P, S], F32, name="bank_b%d" % t) for t in range(PACK)]

        x2_s = pick("x2_s", x_s, two_l, U8)
        x2_w = pick("x2_w", x_w, two_l, U32)
        w2_d = sb("w2_d", [P, H], U32)
        deal(nc, w2_d[:], w2_w[:])
        ws_d = sb("ws_d", [P, H], U8)
        deal(nc, ws_d[:], w_s[:])
        for t in range(PACK):
            product(banks_a, w2_d, ws_d, x2_w[:], x2_s[:], 0, S, t)

        x1_s = pick("x1_s", x_s, offs_l, U8)
        x1_w = pick("x1_w", x_w, offs_l, U32)
        w1_d = sb("w1_d", [P, H], U32)
        deal(nc, w1_d[:], w1_w[:])
        half_gs = sb("half_gs", [P, PACK], F32)
        nc.vector.tensor_scalar(out=half_gs[:], in0=gs_t[:], scalar1=-0.5, scalar2=0.0, op0=ALU.mult, op1=ALU.add)
        for t in range(PACK):
            product(banks_b, w1_d, ws_d[4:P, :], x1_w[:], x1_s[:], 0, S, t)
        win = [sb("win%d" % t, [P, 2 * S], F32) for t in range(PACK)]

        def gate(t):
            nc.scalar.activation(out=d_win[t][:, :S], in_=banks_a[t][:], func=ACT.Copy)
            nc.scalar.activation(out=win[t][:, S:], in_=d_win[t][:].indirect(n2_l[:]), func=ACT.Sigmoid)

        def fetch_y(t):
            nc.scalar.activation(out=win[t][:, :S], in_=banks_b[t][:], func=ACT.Copy, scale=half_gs[:, t : t + 1])

        gate(0)
        gate(1)
        fetch_y(0)
        fetch_y(1)
        for t in (2, 3):
            gate(t)
            fetch_y(t)

        c_sg = pick("c_sg", d_s, k1_l, U8)
        c_sd = sb("c_sd", [P, H], U8)
        deal(nc, c_sd[:], c_sg[:])
        for r in range(4):
            src = 16 * (r // 2) + r % 2
            nc.sync.dma_start(out=c_s[r:P:32, :].bitcast(I32), in_=c_sd[src:P:32, :].bitcast(I32))
        c_wg = pick("c_wg", d_w, k1_l, U32)
        c_w = sb("c_w", [P, H], U32)
        deal(nc, c_w[:], c_wg[:])

        mid = S // 2
        halves = ((0, mid), (mid, S))
        copies = (nc.scalar.copy, nc.vector.tensor_copy)

        def quantise_half(name, src, h, words, scales, tag=None):
            lo, hi = halves[h]
            grouped = sb("%s_bf%d" % (name, h), [P, mid * PACK], BF16, tag=tag)
            copies[h](
                out=grouped[:].rearrange("p (c i t) -> p c t i", i=4, t=PACK),
                in_=src[:, :, lo:hi].rearrange("p t (c i) -> p c t i", i=4),
            )
            nc.vector.quantize_mx(out=words.bitcast(FP8X4), scales=scales, in_=grouped[:])

        z_f = sb("z_f", [P, PACK, S], F32)
        gated = sb("gated", [P, PACK, S], F32, tag="c_wg")

        def gate_y(t):
            nc.vector.scalar_tensor_tensor(
                out=gated[:, t, :], in0=banks_b[t][:], scalar=gs_t[:, t : t + 1], in1=win[t][:, S:],
                op0=ALU.mult, op1=ALU.mult,
            )

        def mix(t, lo, hi):
            nc.vector.tensor_tensor(
                out=z_f[:, t, lo:hi], in0=win[t][:].indirect(entries(n1_l, lo, hi)), in1=gated[:, t, lo:hi], op=ALU.add
            )

        h_win = d_win
        h_own = [sb("h_own%d" % t, [P, S], F32) for t in range(PACK)]

        last = PACK - 1
        for t in range(last):
            gate_y(t)
            mix(t, 0, S)
        gate_y(last)
        z_w = sb("z_w", [P, S], U32)
        z_s = sb("z_s", [P, S], U8)
        for h, (lo, hi) in enumerate(halves):
            mix(last, lo, hi)
            quantise_half("z", z_f, h, z_w[:, lo:hi], z_s[:, lo:hi])
        product(banks_a, c_w, c_s, z_w[:, :mid], z_s[:, :mid], 0, mid, 0)
        product(banks_b, c_w, c_s, z_w[:, mid:], z_s[:, mid:], mid, S, 0)
        for dst in (h_win[0], h_own[0]):
            nc.scalar.activation(out=dst[:, :mid], in_=banks_a[0][:, :mid], func=ACT.Copy, scale=0.0625)
            nc.vector.tensor_scalar(
                out=dst[:, mid:S], in0=banks_b[0][:, mid:], scalar1=0.0625, scalar2=None, op0=ALU.mult
            )
        for t in range(1, PACK):
            product(banks_a, c_w, c_s, z_w[:], z_s[:], 0, S, t)
            for dst in (h_win[t], h_own[t]):
                nc.scalar.activation(out=dst[:, :S], in_=banks_a[t][:], func=ACT.Copy, scale=0.0625)

        out_rows = out_0.rearrange("(p t) j -> p t j", t=PACK)
        out_words = words_view(out_1)
        first = sb("first", [P, PACK, S], F32)
        second = sb("second", [P, PACK, S], F32)
        o_f = sb("o_f", [P, PACK, S], F32)
        o_s = sb("o_s", [P, S], U8)

        def differences(t, lo, hi):
            for dst, offsets in ((first, n3_l), (second, n4_l)):
                nc.vector.tensor_tensor(
                    out=dst[:, t, lo:hi], in0=h_win[t][:].indirect(entries(offsets, lo, hi)),
                    in1=h_own[t][:, lo:hi], op=ALU.subtract,
                )

        def result(t, lo, hi):
            nc.vector.scalar_tensor_tensor(
                out=o_f[:, t, lo:hi], in0=first[:, t, lo:hi], scalar=0.75, in1=second[:, t, lo:hi],
                op0=ALU.mult, op1=ALU.mult,
            )
            nc.sync.dma_start(out=out_rows[:, t, lo:hi], in_=o_f[:, t, lo:hi])

        def planes(h):
            lo, hi = halves[h]
            o_w = sb("o_w%d" % h, [P, mid], U32)
            quantise_half("o", o_f, h, o_w[:], o_s[:, lo:hi], tag="o_bf")
            nc.sync.dma_start(out=out_words[:, lo:hi], in_=o_w[:].bitcast(I32))

        differences(0, mid, S)
        differences(0, 0, mid)
        for t in range(1, last):
            differences(t, 0, S)
            result(t - 1, 0, S)
        differences(last, 0, mid)
        result(last - 1, 0, S)
        result(last, 0, mid)
        planes(0)
        differences(last, mid, S)
        result(last, mid, S)
        planes(1)
        for q in range(4):
            queue = nc.scalar if q % 2 else nc.sync
            queue.dma_start(
                out=out_2[0, 4 * q : 4 * q + 4, :].bitcast(I32), in_=o_s[32 * q : 32 * q + 4, :].bitcast(I32)
            )
